import numpy as np
CORES = [8,9,10,11,12,13,14,15,136,137,138,139,140,141,142,143]
N = 16
ROOT = 12
def setup_inputs(rng):
    return {"x": rng.standard_normal((N, 128, 2048), dtype=np.float32)}
def reference(x):
    y = np.full(x.shape, np.nan, x.dtype)
    y[ROOT] = x.sum(axis=0, dtype=np.float64).astype(x.dtype)
    return {"y": y}

@@ -1,0 +1,104 @@
+from concourse.bass import DstId, RemoteDMATransfer
+from concourse.mybir import AluOpType
+
+ROWS = (32, 32, 32, 32)
+K = len(ROWS)
+ORDER_A = "L0 L1 S0 L2 S1 F0 L3 S2 F1 S3 F2 F3"
+ORDER_B = "L0 L1 S0 L2 S1 F0 L3 S2 F1 S3 F2 F3"
+
+SCRATCH = {
+    "xs0": ("dram", [8, 128, 2 * ROWS[0]], "float32"), "rb0": ("dram", [14, 128, 2 * ROWS[0]], "float32"),
+    "xs1": ("dram", [8, 128, 2 * ROWS[1]], "float32"), "rb1": ("dram", [14, 128, 2 * ROWS[1]], "float32"),
+    "xs2": ("dram", [8, 128, 2 * ROWS[2]], "float32"), "rb2": ("dram", [14, 128, 2 * ROWS[2]], "float32"),
+    "xs3": ("dram", [8, 128, 2 * ROWS[3]], "float32"), "rb3": ("dram", [14, 128, 2 * ROWS[3]], "float32"),
+}
+SEMAPHORES = ["ld0", "ld1", "ld2", "ld3", "arr0", "arr1", "arr2", "arr3", "sent", "own", "fin"]
+
+
+def rank_program(g, core, T, topo):
+    if T.rank_of(core) is None:
+        return
+    XS = [T.xs0, T.xs1, T.xs2, T.xs3]
+    RB = [T.rb0, T.rb1, T.rb2, T.rb3]
+    LD = [T.sem.ld0, T.sem.ld1, T.sem.ld2, T.sem.ld3]
+    ARR = [T.sem.arr0, T.sem.arr1, T.sem.arr2, T.sem.arr3]
+    root = T.cores[12]
+    rl = root % 8
+    hb = root - rl
+    ha = min(c - c % 8 for c in T.cores if c - c % 8 != hb)
+    loc = core % 8
+    on_a = core - loc == ha
+    row0 = [sum(ROWS[:k]) for k in range(K)]
+
+    def owner_a(k, s):
+        if s // 4 == rl // 4:
+            return ha + 4 * (s // 4) + (s % 4 + k) % 4
+        return ha + s
+
+    def dst_id(d):
+        rid, pid = topo.addr(d, core)
+        return DstId(rid=rid, pnc=pid)
+
+    if core == root:
+        g.dma_start(T.y[:, :], T.x[:, :]).then_inc(T.sem.own, 16)
+        g.wait_ge(T.sem.own, 16)
+        for k in range(K):
+            g.wait_ge(ARR[k], 7 * 16 + 8)
+            g.dma_start(T.y[row0[k]:row0[k] + ROWS[k], :], RB[k][0:8], accum_op=AluOpType.add,
+                        max_dma_last_dim=8192).then_inc(T.sem.fin, 16)
+        g.wait_ge(T.sem.fin, 16 * K)
+        return
+
+    sent = [0]
+
+    def load(k):
+        g.dma_start(XS[k][:], T.x[row0[k]:row0[k] + ROWS[k], :]).then_inc(LD[k], 16)
+
+    def scatter(k):
+        g.wait_ge(LD[k], 16)
+        trs = []
+        eng = 2 if on_a else 4
+        for s in range(8):
+            d = owner_a(k, s) if (on_a or s == rl) else hb + s
+            if d == core:
+                continue
+            if on_a:
+                idx = (loc - d % 8 - 1) % 8
+                mask = 3 << eng
+                eng += 2
+            elif s == rl:
+                idx = 7 + (loc if loc < rl else loc - 1)
+                mask = 0xF
+            else:
+                idx = [j for j in range(8) if j != rl and j != d % 8].index(loc)
+                mask = 3 << eng
+                eng += 2
+            trs.append(RemoteDMATransfer(dst_ids=[dst_id(d)], dma_engine_mask=mask, remote_sem=ARR[k],
+                                         src=XS[k][s], dst=RB[k][idx]))
+            sent[0] += 4 if mask == 0xF else 2
+        g.remote_dma_fused(trs, local_sem=T.sem.sent)
+
+    def fold(k):
+        if on_a:
+            s = [t for t in range(8) if owner_a(k, t) == core][0]
+            n = 14 if s == rl else 7
+            g.wait_ge(ARR[k], 7 * 2 + (7 * 4 if s == rl else 0))
+            d, out, mask, ne = (root, RB[k][s], 0xFF, 8) if s == rl else (hb + s, RB[k][6], 0xFF, 8)
+        else:
+            s, n = loc, 7
+            g.wait_ge(ARR[k], 6 * 2 + 8)
+            d, out, mask, ne = root, RB[k][s], 0xFFFF, 16
+        g.remote_dma_fused([RemoteDMATransfer(dst_ids=[dst_id(d)], dma_engine_mask=mask, remote_sem=ARR[k],
+                                              srcs=[XS[k][s]] + [RB[k][i] for i in range(n)], dsts=[out], alu_op=1)],
+                           local_sem=T.sem.sent)
+        sent[0] += ne
+
+    for op in (ORDER_A if on_a else ORDER_B).split():
+        k = int(op[1:])
+        if op[0] == "L":
+            load(k)
+        elif op[0] == "S":
+            scatter(k)
+        else:
+            fold(k)
+    g.wait_ge(T.sem.sent, sent[0])

@@ -3,8 +3,8 @@ from concourse.mybir import AluOpType
 
 ROWS = (32, 32, 32, 32)
 K = len(ROWS)
-ORDER_A = "L0 L1 S0 L2 S1 F0 L3 S2 F1 S3 F2 F3"
-ORDER_B = "L0 L1 S0 L2 S1 F0 L3 S2 F1 S3 F2 F3"
+ORDER_A = "L0 L1 L2 L3 S0 S1 S2 S3 F0 F1 F2 F3"
+ORDER_B = "L0 L1 L2 L3 S0 S1 S2 S3 F0 F1 F2 F3"
 
 SCRATCH = {
     "xs0": ("dram", [8, 128, 2 * ROWS[0]], "float32"), "rb0": ("dram", [14, 128, 2 * ROWS[0]], "float32"),

@@ -1,16 +1,13 @@
 from concourse.bass import DstId, RemoteDMATransfer
 from concourse.mybir import AluOpType
 
-ROWS = (32, 32, 32, 32)
-K = len(ROWS)
-ORDER_A = "L0 L1 L2 L3 S0 S1 S2 S3 F0 F1 F2 F3"
-ORDER_B = "L0 L1 L2 L3 S0 S1 S2 S3 F0 F1 F2 F3"
+K = 4
+R = 128 // K
+W = 2 * R
 
 SCRATCH = {
-    "xs0": ("dram", [8, 128, 2 * ROWS[0]], "float32"), "rb0": ("dram", [14, 128, 2 * ROWS[0]], "float32"),
-    "xs1": ("dram", [8, 128, 2 * ROWS[1]], "float32"), "rb1": ("dram", [14, 128, 2 * ROWS[1]], "float32"),
-    "xs2": ("dram", [8, 128, 2 * ROWS[2]], "float32"), "rb2": ("dram", [14, 128, 2 * ROWS[2]], "float32"),
-    "xs3": ("dram", [8, 128, 2 * ROWS[3]], "float32"), "rb3": ("dram", [14, 128, 2 * ROWS[3]], "float32"),
+    "xs": ("dram", [8 * K, 128, W], "float32"),
+    "rb": ("dram", [14 * K, 128, W], "float32"),
 }
 SEMAPHORES = ["ld0", "ld1", "ld2", "ld3", "arr0", "arr1", "arr2", "arr3", "sent", "own", "fin"]
 
@@ -18,8 +15,6 @@ SEMAPHORES = ["ld0", "ld1", "ld2", "ld3", "arr0", "arr1", "arr2", "arr3", "sent"
 def rank_program(g, core, T, topo):
     if T.rank_of(core) is None:
         return
-    XS = [T.xs0, T.xs1, T.xs2, T.xs3]
-    RB = [T.rb0, T.rb1, T.rb2, T.rb3]
     LD = [T.sem.ld0, T.sem.ld1, T.sem.ld2, T.sem.ld3]
     ARR = [T.sem.arr0, T.sem.arr1, T.sem.arr2, T.sem.arr3]
     root = T.cores[12]
@@ -28,7 +23,6 @@ def rank_program(g, core, T, topo):
     ha = min(c - c % 8 for c in T.cores if c - c % 8 != hb)
     loc = core % 8
     on_a = core - loc == ha
-    row0 = [sum(ROWS[:k]) for k in range(K)]
 
     def owner_a(k, s):
         if s // 4 == rl // 4:
@@ -39,66 +33,73 @@ def rank_program(g, core, T, topo):
         rid, pid = topo.addr(d, core)
         return DstId(rid=rid, pnc=pid)
 
+    def plan(q):
+        ql, qa = q % 8, q - q % 8 == ha
+        pieces = []
+        for k in range(K):
+            for s in range(8):
+                d = owner_a(k, s) if (qa or s == rl) else hb + s
+                if d == q:
+                    continue
+                if qa:
+                    idx = (ql - d % 8 - 1) % 8
+                elif s == rl:
+                    idx = 7 + (ql if ql < rl else ql - 1)
+                else:
+                    idx = [j for j in range(8) if j != rl and j != d % 8].index(ql)
+                pieces.append((k, s, d, idx))
+        calls = []
+        for i in range(0, len(pieces), 8):
+            grp = pieces[i:i + 8]
+            ne = 16 // len(grp)
+            grp = sorted(grp, key=lambda p: p[2] - p[2] % 8 == q - ql)
+            calls.append([p + (((1 << ne) - 1) << (ne * j), ne) for j, p in enumerate(grp)])
+        return calls
+
     if core == root:
         g.dma_start(T.y[:, :], T.x[:, :]).then_inc(T.sem.own, 16)
         g.wait_ge(T.sem.own, 16)
         for k in range(K):
             g.wait_ge(ARR[k], 7 * 16 + 8)
-            g.dma_start(T.y[row0[k]:row0[k] + ROWS[k], :], RB[k][0:8], accum_op=AluOpType.add,
+            g.dma_start(T.y[R * k:R * (k + 1), :], T.rb[14 * k:14 * k + 8], accum_op=AluOpType.add,
                         max_dma_last_dim=8192).then_inc(T.sem.fin, 16)
         g.wait_ge(T.sem.fin, 16 * K)
         return
 
-    sent = [0]
+    lands = [0] * K
+    for q in T.cores:
+        if q != root and q != core:
+            for call in plan(q):
+                for (k, s, d, idx, mask, ne) in call:
+                    if d == core:
+                        lands[k] += ne
+    sent = 0
 
-    def load(k):
-        g.dma_start(XS[k][:], T.x[row0[k]:row0[k] + ROWS[k], :]).then_inc(LD[k], 16)
+    for k in range(K):
+        g.dma_start(T.xs[8 * k:8 * (k + 1)], T.x[R * k:R * (k + 1), :]).then_inc(LD[k], 16)
 
-    def scatter(k):
-        g.wait_ge(LD[k], 16)
-        trs = []
-        eng = 2 if on_a else 4
-        for s in range(8):
-            d = owner_a(k, s) if (on_a or s == rl) else hb + s
-            if d == core:
-                continue
-            if on_a:
-                idx = (loc - d % 8 - 1) % 8
-                mask = 3 << eng
-                eng += 2
-            elif s == rl:
-                idx = 7 + (loc if loc < rl else loc - 1)
-                mask = 0xF
-            else:
-                idx = [j for j in range(8) if j != rl and j != d % 8].index(loc)
-                mask = 3 << eng
-                eng += 2
-            trs.append(RemoteDMATransfer(dst_ids=[dst_id(d)], dma_engine_mask=mask, remote_sem=ARR[k],
-                                         src=XS[k][s], dst=RB[k][idx]))
-            sent[0] += 4 if mask == 0xF else 2
-        g.remote_dma_fused(trs, local_sem=T.sem.sent)
+    have = 0
+    for call in plan(core):
+        while have <= max(p[0] for p in call):
+            g.wait_ge(LD[have], 16)
+            have += 1
+        g.remote_dma_fused([RemoteDMATransfer(dst_ids=[dst_id(d)], dma_engine_mask=mask, remote_sem=ARR[k],
+                                              src=T.xs[8 * k + s], dst=T.rb[14 * k + idx])
+                            for (k, s, d, idx, mask, ne) in call], local_sem=T.sem.sent)
+        sent += 16
 
-    def fold(k):
+    for k in range(K):
         if on_a:
             s = [t for t in range(8) if owner_a(k, t) == core][0]
             n = 14 if s == rl else 7
-            g.wait_ge(ARR[k], 7 * 2 + (7 * 4 if s == rl else 0))
-            d, out, mask, ne = (root, RB[k][s], 0xFF, 8) if s == rl else (hb + s, RB[k][6], 0xFF, 8)
+            g.wait_ge(ARR[k], lands[k])
+            d, out, mask, ne = (root, T.rb[14 * k + s], 0xFF, 8) if s == rl else (hb + s, T.rb[14 * k + 6], 0xFF, 8)
         else:
             s, n = loc, 7
-            g.wait_ge(ARR[k], 6 * 2 + 8)
-            d, out, mask, ne = root, RB[k][s], 0xFFFF, 16
+            g.wait_ge(ARR[k], lands[k] + 8)
+            d, out, mask, ne = root, T.rb[14 * k + s], 0xFFFF, 16
         g.remote_dma_fused([RemoteDMATransfer(dst_ids=[dst_id(d)], dma_engine_mask=mask, remote_sem=ARR[k],
-                                              srcs=[XS[k][s]] + [RB[k][i] for i in range(n)], dsts=[out], alu_op=1)],
-                           local_sem=T.sem.sent)
-        sent[0] += ne
-
-    for op in (ORDER_A if on_a else ORDER_B).split():
-        k = int(op[1:])
-        if op[0] == "L":
-            load(k)
-        elif op[0] == "S":
-            scatter(k)
-        else:
-            fold(k)
-    g.wait_ge(T.sem.sent, sent[0])
+                                              srcs=[T.xs[8 * k + s]] + [T.rb[14 * k + i] for i in range(n)], dsts=[out],
+                                              alu_op=1)], local_sem=T.sem.sent)
+        sent += ne
+    g.wait_ge(T.sem.sent, sent)

@@ -1,15 +1,15 @@
 from concourse.bass import DstId, RemoteDMATransfer
-from concourse.mybir import AluOpType
 
 K = 4
 R = 128 // K
 W = 2 * R
+NS = 15
 
 SCRATCH = {
     "xs": ("dram", [8 * K, 128, W], "float32"),
-    "rb": ("dram", [14 * K, 128, W], "float32"),
+    "rb": ("dram", [NS * K, 128, W], "float32"),
 }
-SEMAPHORES = ["ld0", "ld1", "ld2", "ld3", "arr0", "arr1", "arr2", "arr3", "sent", "own", "fin"]
+SEMAPHORES = ["ld0", "ld1", "ld2", "ld3", "arr0", "arr1", "arr2", "arr3", "sent", "fin"]
 
 
 def rank_program(g, core, T, topo):
@@ -44,9 +44,9 @@ def rank_program(g, core, T, topo):
                 if qa:
                     idx = (ql - d % 8 - 1) % 8
                 elif s == rl:
-                    idx = 7 + (ql if ql < rl else ql - 1)
+                    idx = 7 + ql
                 else:
-                    idx = [j for j in range(8) if j != rl and j != d % 8].index(ql)
+                    idx = [j for j in range(8) if j != d % 8].index(ql)
                 pieces.append((k, s, d, idx))
         calls = []
         for i in range(0, len(pieces), 8):
@@ -56,19 +56,9 @@ def rank_program(g, core, T, topo):
             calls.append([p + (((1 << ne) - 1) << (ne * j), ne) for j, p in enumerate(grp)])
         return calls
 
-    if core == root:
-        g.dma_start(T.y[:, :], T.x[:, :]).then_inc(T.sem.own, 16)
-        g.wait_ge(T.sem.own, 16)
-        for k in range(K):
-            g.wait_ge(ARR[k], 7 * 16 + 8)
-            g.dma_start(T.y[R * k:R * (k + 1), :], T.rb[14 * k:14 * k + 8], accum_op=AluOpType.add,
-                        max_dma_last_dim=8192).then_inc(T.sem.fin, 16)
-        g.wait_ge(T.sem.fin, 16 * K)
-        return
-
     lands = [0] * K
     for q in T.cores:
-        if q != root and q != core:
+        if q != core:
             for call in plan(q):
                 for (k, s, d, idx, mask, ne) in call:
                     if d == core:
@@ -84,22 +74,30 @@ def rank_program(g, core, T, topo):
             g.wait_ge(LD[have], 16)
             have += 1
         g.remote_dma_fused([RemoteDMATransfer(dst_ids=[dst_id(d)], dma_engine_mask=mask, remote_sem=ARR[k],
-                                              src=T.xs[8 * k + s], dst=T.rb[14 * k + idx])
+                                              src=T.xs[8 * k + s], dst=T.rb[NS * k + idx])
                             for (k, s, d, idx, mask, ne) in call], local_sem=T.sem.sent)
         sent += 16
+
+    if core == root:
+        for k in range(K):
+            g.wait_ge(ARR[k], 7 * 16 + 8)
+            g.dma_start(T.y[R * k:R * (k + 1), :], T.rb[NS * k:NS * k + 8]).then_inc(T.sem.fin, 16)
+        g.wait_ge(T.sem.fin, 16 * K)
+        g.wait_ge(T.sem.sent, sent)
+        return
 
     for k in range(K):
         if on_a:
             s = [t for t in range(8) if owner_a(k, t) == core][0]
-            n = 14 if s == rl else 7
+            n = 15 if s == rl else 7
             g.wait_ge(ARR[k], lands[k])
-            d, out, mask, ne = (root, T.rb[14 * k + s], 0xFF, 8) if s == rl else (hb + s, T.rb[14 * k + 6], 0xFF, 8)
+            d, out, mask, ne = (root, T.rb[NS * k + s], 0xFF, 8) if s == rl else (hb + s, T.rb[NS * k + 7], 0xFF, 8)
         else:
-            s, n = loc, 7
+            s, n = loc, 8
             g.wait_ge(ARR[k], lands[k] + 8)
-            d, out, mask, ne = root, T.rb[14 * k + s], 0xFFFF, 16
+            d, out, mask, ne = root, T.rb[NS * k + s], 0xFFFF, 16
         g.remote_dma_fused([RemoteDMATransfer(dst_ids=[dst_id(d)], dma_engine_mask=mask, remote_sem=ARR[k],
-                                              srcs=[T.xs[8 * k + s]] + [T.rb[14 * k + i] for i in range(n)], dsts=[out],
+                                              srcs=[T.xs[8 * k + s]] + [T.rb[NS * k + i] for i in range(n)], dsts=[out],
                                               alu_op=1)], local_sem=T.sem.sent)
         sent += ne
     g.wait_ge(T.sem.sent, sent)

from concourse.bass import DstId, RemoteDMATransfer

K = 4
R = 128 // K
W = 2 * R
NS = 15

SCRATCH = {
    "xs": ("dram", [8 * K, 128, W], "float32"),
    "rb": ("dram", [NS * K, 128, W], "float32"),
}
SEMAPHORES = ["ld0", "ld1", "ld2", "ld3", "arr0", "arr1", "arr2", "arr3", "sent", "fin"]


def rank_program(g, core, T, topo):
    if T.rank_of(core) is None:
        return
    LD = [T.sem.ld0, T.sem.ld1, T.sem.ld2, T.sem.ld3]
    ARR = [T.sem.arr0, T.sem.arr1, T.sem.arr2, T.sem.arr3]
    root = T.cores[12]
    rl = root % 8
    hb = root - rl
    ha = min(c - c % 8 for c in T.cores if c - c % 8 != hb)
    loc = core % 8
    on_a = core - loc == ha

    def owner_a(k, s):
        if s // 4 == rl // 4:
            return ha + 4 * (s // 4) + (s % 4 + k) % 4
        return ha + s

    def dst_id(d):
        rid, pid = topo.addr(d, core)
        return DstId(rid=rid, pnc=pid)

    def plan(q):
        ql, qa = q % 8, q - q % 8 == ha
        pieces = []
        for k in range(K):
            for s in range(8):
                d = owner_a(k, s) if (qa or s == rl) else hb + s
                if d == q:
                    continue
                if qa:
                    idx = (ql - d % 8 - 1) % 8
                elif s == rl:
                    idx = 7 + ql
                else:
                    idx = [j for j in range(8) if j != d % 8].index(ql)
                pieces.append((k, s, d, idx))
        calls = []
        for i in range(0, len(pieces), 8):
            grp = pieces[i:i + 8]
            ne = 16 // len(grp)
            grp = sorted(grp, key=lambda p: p[2] - p[2] % 8 == q - ql)
            calls.append([p + (((1 << ne) - 1) << (ne * j), ne) for j, p in enumerate(grp)])
        return calls

    lands = [0] * K
    for q in T.cores:
        if q != core:
            for call in plan(q):
                for (k, s, d, idx, mask, ne) in call:
                    if d == core:
                        lands[k] += ne
    sent = 0

    for k in range(K):
        g.dma_start(T.xs[8 * k:8 * (k + 1)], T.x[R * k:R * (k + 1), :]).then_inc(LD[k], 16)

    have = 0
    for call in plan(core):
        while have <= max(p[0] for p in call):
            g.wait_ge(LD[have], 16)
            have += 1
        g.remote_dma_fused([RemoteDMATransfer(dst_ids=[dst_id(d)], dma_engine_mask=mask, remote_sem=ARR[k],
                                              src=T.xs[8 * k + s], dst=T.rb[NS * k + idx])
                            for (k, s, d, idx, mask, ne) in call], local_sem=T.sem.sent)
        sent += 16

    if core == root:
        for k in range(K):
            g.wait_ge(ARR[k], 7 * 16 + 8)
            g.dma_start(T.y[R * k:R * (k + 1), :], T.rb[NS * k:NS * k + 8]).then_inc(T.sem.fin, 16)
        g.wait_ge(T.sem.fin, 16 * K)
        g.wait_ge(T.sem.sent, sent)
        return

    for k in range(K):
        if on_a:
            s = [t for t in range(8) if owner_a(k, t) == core][0]
            n = 15 if s == rl else 7
            g.wait_ge(ARR[k], lands[k])
            d, out, mask, ne = (root, T.rb[NS * k + s], 0xFF, 8) if s == rl else (hb + s, T.rb[NS * k + 7], 0xFF, 8)
        else:
            s, n = loc, 8
            g.wait_ge(ARR[k], lands[k] + 8)
            d, out, mask, ne = root, T.rb[NS * k + s], 0xFFFF, 16
        g.remote_dma_fused([RemoteDMATransfer(dst_ids=[dst_id(d)], dma_engine_mask=mask, remote_sem=ARR[k],
                                              srcs=[T.xs[8 * k + s]] + [T.rb[NS * k + i] for i in range(n)], dsts=[out],
                                              alu_op=1)], local_sem=T.sem.sent)
        sent += ne
    g.wait_ge(T.sem.sent, sent)
